import numpy as np, ml_dtypes
CORES = [25,29,65,69,153,157,193,197]
N = 8
import mx_ref
BF = ml_dtypes.bfloat16
def entries(a):
    return np.ascontiguousarray(a.T).reshape(-1)
def table(e):
    return np.ascontiguousarray(np.reshape(e, (-1, 16)).T).astype(np.int32)
def cols(t, e):
    v = np.concatenate([t.reshape(128, -1, 4), np.zeros((128, 1, 4), BF)], axis=1)
    return np.ascontiguousarray(v[:, e]).reshape(128, -1)
def f(rng, *shape):
    return mx_ref.flush((rng.standard_normal(shape, dtype=np.float32) * np.exp2(rng.integers(-2, 3, shape[:-1] + (1,)))).astype(BF))
def wide(rng, *shape, cols=0):
    v = rng.standard_normal(shape, dtype=np.float32) * np.exp2(rng.integers(-12, 13, shape)).astype(np.float32)
    if cols: v *= np.repeat(np.exp2(rng.integers(-cols, cols + 1, shape[:-2] + (1, shape[-1] // 4))) * (rng.random(shape[:-2] + (1, shape[-1] // 4)) > 0.0625), 4, axis=-1).astype(np.float32)
    return mx_ref.flush(v.astype(BF))
T, KP, TOT, QT = 256, 160, 1024, 8
CAPP, DR, CW = KP // N, T // 16, TOT // N
def counts(rng, lo, hi):
    L, U = [TOT], [TOT]
    for q in range(N)[::-1]:
        L.insert(0, max(q * CW - N * DR, L[0] - hi[q]))
        U.insert(0, min((q - 1) * CW + N * (DR + CAPP + 1), U[0] - lo[q]))
    n, s = [], 0
    for q in range(N):
        n.append(int(rng.integers(max(lo[q], L[q + 1] - s), min(hi[q], U[q + 1] - s) + 1))); s += n[-1]
    return n
def slots(k):
    s, p, g = np.full((N, N, CAPP), -1), np.zeros((N, CW), int), 0
    for q in range(N):
        used = [0] * N
        for c in k[q]:
            r = g % N
            s[q, r, used[r]] = c; p[r, g // N] = q * CAPP + used[r]
            used[r] += 1; g += 1
    return np.stack([table(a) for a in s]), np.stack([table(a) for a in p])
def lists(rng, lo=None, hi=None, front=False):
    n = counts(rng, [3 * T // 8] * N if lo is None else lo, [KP] * N if hi is None else hi)
    k = [np.arange(m) if front else np.sort(rng.choice(T, m, replace=False)) for m in n]
    s, p = slots(k)
    return {"kept": np.stack([table(np.concatenate([a, np.full(KP - len(a), -1)])) for a in k]), "snd": s, "pl": p}
def setup_inputs(rng):
    return {"x": f(rng, N, 128, 4 * T), "qw": f(rng, N, 128, QT * 512), **lists(rng)}
def setup_inputs_few(rng):
    return {**setup_inputs(rng), **lists(rng, [T // 2] * (N - 1) + [1], [KP] * (N - 1) + [N])}
def setup_inputs_front(rng):
    return {**setup_inputs(rng), **lists(rng, front=True)}
def setup_inputs_none(rng):
    return {**setup_inputs(rng), **lists(rng, [0] + [T // 2] * (N - 1), [0] + [KP] * (N - 1))}
def setup_inputs_spread(rng):
    d = setup_inputs(rng); d["x"] = wide(rng, N, 128, 4 * T); return d
def setup_inputs_steep(rng):
    d = {**setup_inputs(rng), **lists(rng, [KP] * 5 + [CW + 1, 1, 1], [KP] * 5 + [CW + N, KP, KP])}
    assert (int((d["kept"][:6] >= 0).sum()) - 1) // N - 5 * (CW // N) == DR + CAPP
    return d
def check_inputs(d):
    b, k = [], []
    for q in range(N):
        e = entries(d["kept"][q]); n = int((e >= 0).sum()); k.append(e[:n])
        if e.min() < -1 or e.max() >= T or (e[:n] < 0).any() or (e[n:] != -1).any() or (np.diff(e[:n]) <= 0).any(): b.append("kept")
    if sum(len(a) for a in k) != TOT: b.append("sum of n_q")
    if b: return b
    g = 0
    for q in range(N):
        a = np.arange(g, g + len(k[q])); g += len(k[q])
        if len(a) == 0: continue
        if np.bincount(a % N).max() > CAPP: b.append("columns of a pair")
        p = a // N - q * TOT // (N * N)
        if p.min() < -DR or p.max() > DR + CAPP: b.append("drift")
    s, p = slots(k)
    if not np.array_equal(s, d["snd"]): b.append("snd")
    if not np.array_equal(p, d["pl"]): b.append("pl")
    return b
def reference(x, qw, kept, snd, pl):
    v = []
    for q in range(N):
        e = entries(kept[q]); v.append(cols(x[q], e[e >= 0]))
    v = np.concatenate(v, axis=1)
    y = np.zeros((N, 128, QT * CW), np.float32)
    for r in range(N):
        C = mx_ref.quantize(cols(v, np.arange(r, TOT, N)))
        for o in range(QT): y[r][:, CW * o:CW * o + CW] = mx_ref.matmul(mx_ref.quantize(qw[r][:, 512 * o:512 * o + 512]), C)
    return {"y": y}

@@ -1,0 +1,237 @@
+from concourse.bass import DstId, RemoteDMATransfer
+from concourse.mybir import dt, AluOpType, ActivationFunctionType
+
+N = 8
+KP = 160
+CAPP = KP // N
+CW = 128
+QT = 8
+PAD = 128 - CAPP
+NE = 128 + (N - 1) * CAPP
+
+SCRATCH = {
+    "L": ("sbuf", [128, KP // 16], "int32"),
+    "U": ("sbuf", [128, 4 * (KP // 16)], "uint16"),
+    "X": ("sbuf", [128, 1024], "bfloat16"),
+    "H": ("sbuf", [128, 4 * (PAD + KP)], "bfloat16"),
+    "WQ": ("sbuf", [128, QT * 512], "bfloat16"),
+    "WC": ("sbuf", [128, QT * 128], "float8_e4m3fn_x4"),
+    "WS": ("sbuf", [128, QT * 128], "uint8"),
+    "QC": ("sbuf", [128, KP], "float8_e4m3fn_x4"),
+    "QS": ("sbuf", [128, KP], "uint8"),
+    "EC": ("sbuf", [128, NE], "float8_e4m3fn_x4"),
+    "ES": ("sbuf", [128, NE], "uint8"),
+    "RC": ("sbuf", [128, 2 * CAPP], "float8_e4m3fn_x4"),
+    "RS": ("sbuf", [128, 2 * CAPP], "uint8"),
+    "PLI": ("sbuf", [128, CW // 16], "int32"),
+    "TM": ("sbuf", [128, N * (CW // 16)], "int32"),
+    "AC": ("sbuf", [128, (N + 1) * (CW // 16)], "int32"),
+    "V": ("sbuf", [128, 2 * (CW // 16)], "uint16"),
+    "S": ("sbuf", [128, QT * KP], "float32"),
+    "YS": ("sbuf", [128, QT * CW], "float32"),
+    "P": ("psum", [128, QT * 512], "float32"),
+}
+SEMAPHORES = ["lst", "xin", "qa", "qb", "pls", "vz", "vl", "vg", "sg", "qx", "ex", "wq", "vp", "sent", "loc",
+              "near", "far", "rc", "rs", "em", "ec", "lm", "vc", "sc", "vo", "so", "pv", "st"]
+
+
+def near_far(T, topo, core):
+    near = [q for q in range(N) if T.cores[q] != core and topo.may_write(core, T.cores[q])]
+    far = [q for q in range(N) if T.cores[q] != core and q not in near]
+    groups = []
+    for q in far:
+        if groups and T.cores[q] in topo.cores_of(T.cores[groups[-1][-1]]):
+            groups[-1].append(q)
+        else:
+            groups.append([q])
+    return near, far, groups
+
+
+def relays(T, topo, core, groups):
+    ports = [k for k in topo.cores_of(core) if topo.die(k) == topo.die(core) and T.rank_of(k) is None
+             and topo.may_write(k, T.cores[groups[0][0]])]
+    return ports[:len(groups)]
+
+
+def bits(engines):
+    return sum(1 << e for e in engines)
+
+
+def send(topo, src, dst, engines, sem, frm, to):
+    rid, pid = topo.addr(dst, src)
+    return RemoteDMATransfer(dst_ids=[DstId(rid=rid, pnc=pid)], dma_engine_mask=bits(engines), remote_sem=sem, src=frm, dst=to)
+
+
+def rank_program(g, core, T, topo):
+    rank = T.rank_of(core)
+    if rank is None:
+        for owner in T.cores:
+            if owner in topo.cores_of(core):
+                near, far, groups = near_far(T, topo, owner)
+                ports = relays(T, topo, owner, groups)
+                if core in ports:
+                    relay_program(g, core, T, topo, T.rank_of(owner), groups[ports.index(core)])
+        return
+    owner_program(g, core, T, topo, rank)
+
+
+def relay_program(g, core, T, topo, src, dsts):
+    M = T.sem
+    codes, planes = [], []
+    for i, q in enumerate(dsts):
+        d = T.cores[q]
+        n, f, gr = near_far(T, topo, d)
+        e = topo.engines(core, d)
+        w = len(e) // len(dsts)
+        e = e[i * w:(i + 1) * w]
+        a, b = i * CAPP, 128 + (len(n) + f.index(src)) * CAPP
+        codes.append(send(topo, core, d, e, M.far, T.RC[:, a:a + CAPP].bitcast(dt.uint8), T.EC[:, b:b + CAPP].bitcast(dt.uint8)))
+        planes.append(send(topo, core, d, e, M.far, T.RS[:, a:a + CAPP], T.ES[:, b:b + CAPP]))
+    g.wait_ge(M.rc, 8)
+    g.remote_dma_fused(codes, local_sem=M.loc)
+    g.wait_ge(M.rs, 8)
+    g.remote_dma_fused(planes, local_sem=M.loc)
+    g.wait_ge(M.loc, 16)
+
+
+def owner_program(g, core, T, topo, rank):
+    M = T.sem
+    near, far, groups = near_far(T, topo, core)
+    ports = relays(T, topo, core, groups)
+    K = KP // 16
+    J = CW // 16
+    COPY = ActivationFunctionType.Copy
+
+    for p in range(8):
+        q = g.sync if p < 3 else g.scalar
+        q.dma_start(T.L[16 * p:16 * p + 16, :], T.snd[:, :]).then_inc(M.lst, 16)
+    g.sync.dma_start(T.X[:, :], T.x[:, :]).then_inc(M.xin, 16)
+    g.sync.dma_start(T.WQ[:, 0:2048], T.qw[:, 0:2048]).then_inc(M.qa, 16)
+    for p in range(8):
+        g.scalar.dma_start(T.PLI[16 * p:16 * p + 16, :], T.pl[:, :]).then_inc(M.pls, 16)
+
+    h0 = 4 * PAD
+    h1 = h0 + 4 * KP
+    g.vector.memset(T.H[:, 0:h0], 0.0).then_inc(M.vz, 1)
+    g.vector.wait_ge(M.lst, 128)
+    for t in (2, 3, 0, 1):
+        g.vector.tensor_scalar(T.U[:, K * t:K * t + K], T.L[:, :], 4, t, AluOpType.mult, AluOpType.add).then_inc(M.vl, 1)
+    g.scalar.wait_ge(M.xin, 16)
+    for i, t in enumerate((2, 3)):
+        g.scalar.wait_ge(M.vl, i + 1)
+        g.scalar.activation(T.H[:, h0 + t:h1:4], T.X[:, 0:1024].indirect(T.U[:, K * t:K * t + K]), COPY).then_inc(M.sg, 1)
+    g.vector.wait_ge(M.xin, 16)
+    for i, t in enumerate((0, 1)):
+        g.vector.wait_ge(M.vl, i + 3)
+        g.vector.tensor_copy(T.H[:, h0 + t:h1:4], T.X[:, 0:1024].indirect(T.U[:, K * t:K * t + K])).then_inc(M.vg, 1)
+    g.vector.wait_ge(M.vg, 2)
+    g.vector.wait_ge(M.sg, 2)
+    g.vector.quantize_mx(T.QC[:, 0:KP], T.QS[:, 0:KP], T.H[:, h0:h1]).then_inc(M.qx, 1)
+
+    fc, fs, nc, ns = [], [], [], []
+    for i, gr in enumerate(groups):
+        e = topo.engines(core, ports[i])
+        w = len(e) // len(groups)
+        e = e[i * w:(i + 1) * w]
+        a = gr[0] * CAPP
+        b = a + len(gr) * CAPP
+        fc.append(send(topo, core, ports[i], e, M.rc, T.QC[:, a:b].bitcast(dt.uint8), T.RC[:, 0:b - a].bitcast(dt.uint8)))
+        fs.append(send(topo, core, ports[i], e, M.rs, T.QS[:, a:b], T.RS[:, 0:b - a]))
+    plane = [q for q in near if topo.same_plane(core, T.cores[q])]
+    for q in near:
+        d = T.cores[q]
+        if q in plane:
+            e = topo.engines(core, d)
+            w = len(e) // len(plane)
+            i = plane.index(q)
+            e = e[i * w:(i + 1) * w]
+        else:
+            e = [k for k in topo.engines(core, d) if k not in topo.engines(core, T.cores[plane[0]])]
+        dn = near_far(T, topo, d)[0]
+        a, b = q * CAPP, 128 + dn.index(rank) * CAPP
+        nc.append(send(topo, core, d, e, M.near, T.QC[:, a:a + CAPP].bitcast(dt.uint8), T.EC[:, b:b + CAPP].bitcast(dt.uint8)))
+        ns.append(send(topo, core, d, e, M.near, T.QS[:, a:a + CAPP], T.ES[:, b:b + CAPP]))
+    g.wait_ge(M.qx, 1)
+    g.remote_dma_fused(fc, local_sem=M.loc)
+    g.remote_dma_fused(fs, local_sem=M.loc)
+    g.sem_inc(M.sent, 1)
+    g.remote_dma_fused(nc, local_sem=M.loc)
+    g.remote_dma_fused(ns, local_sem=M.loc)
+    g.wait_ge(M.loc, 64)
+
+    g.sync.wait_ge(M.sent, 1)
+    g.sync.dma_start(T.WQ[:, 2048:4096], T.qw[:, 2048:4096]).then_inc(M.qb, 16)
+
+    s0 = 4 * (rank * CAPP)
+    g.vector.wait_ge(M.vz, 1)
+    g.vector.quantize_mx(T.EC[:, 0:128], T.ES[:, 0:128], T.H[:, s0:s0 + 512]).then_inc(M.ex, 1)
+    g.vector.wait_ge(M.qa, 16)
+    g.vector.quantize_mx(T.WC[:, 0:512], T.WS[:, 0:512], T.WQ[:, 0:2048]).then_inc(M.wq, 1)
+
+    order = [rank] + near + far
+    delta = [CAPP * (order.index(q) - q) for q in range(N)]
+    steps = [(q, delta[q] - delta[q - 1]) for q in range(1, N) if delta[q] != delta[q - 1]]
+    g.vector.wait_ge(M.pls, 128)
+    g.vector.tensor_scalar(T.AC[:, 0:J], T.PLI[:, :], delta[0], None, AluOpType.add).then_inc(M.vp, 1)
+    for i, (q, s) in enumerate(steps):
+        g.vector.tensor_scalar(T.TM[:, J * i:J * i + J], T.PLI[:, :], q * CAPP, s, AluOpType.is_ge, AluOpType.mult).then_inc(M.vp, 1)
+    n = 1 + len(steps)
+    for i in range(len(steps)):
+        g.vector.wait_ge(M.vp, n)
+        g.vector.tensor_tensor(T.AC[:, J * (i + 1):J * (i + 2)], T.AC[:, J * i:J * (i + 1)], T.TM[:, J * i:J * i + J],
+                               AluOpType.add).then_inc(M.vp, 1)
+        n += 1
+    last = T.AC[:, J * len(steps):J * (len(steps) + 1)]
+    g.vector.wait_ge(M.vp, n)
+    g.vector.tensor_scalar(T.V[:, 0:J], last, 0, None, AluOpType.add).then_inc(M.pv, 1)
+    g.vector.tensor_scalar(T.V[:, J:2 * J], last, KP, None, AluOpType.add).then_inc(M.pv, 1)
+    g.vector.wait_ge(M.qb, 16)
+    g.vector.quantize_mx(T.WC[:, 512:1024], T.WS[:, 512:1024], T.WQ[:, 2048:4096]).then_inc(M.wq, 1)
+
+    e0 = 128 + len(near) * CAPP - 128
+    l0 = NE - 128
+    hw = (1 + len(near)) * CAPP
+    fw = len(far) * CAPP
+    g.tensor.wait_ge(M.ex, 1)
+    g.tensor.wait_ge(M.near, 32)
+    for o in range(QT):
+        if o % 4 == 0:
+            g.tensor.wait_ge(M.wq, o // 4 + 1)
+        g.tensor.matmul_mx(T.P[:, 512 * o:512 * o + 128], T.WC[:, 128 * o:128 * o + 128], T.WS[:, 128 * o:128 * o + 128],
+                           T.EC[:, e0:e0 + 128], T.ES[:, e0:e0 + 128], True, True).then_inc(M.em, 1)
+        g.scalar.wait_ge(M.em, o + 1)
+        g.scalar.activation(T.S[:, KP * o:KP * o + hw], T.P[:, 512 * o + 128 - hw:512 * o + 128], COPY).then_inc(M.ec, 1)
+    turn = [0, 4, 1, 5, 2, 6, 3, 7]
+    g.tensor.wait_ge(M.far, 32)
+    g.tensor.wait_ge(M.ec, 8)
+    for o in turn:
+        g.tensor.matmul_mx(T.P[:, 512 * o:512 * o + 128], T.WC[:, 128 * o:128 * o + 128], T.WS[:, 128 * o:128 * o + 128],
+                           T.EC[:, l0:l0 + 128], T.ES[:, l0:l0 + 128], True, True).then_inc(M.lm, 1)
+
+    g.vector.wait_ge(M.ec, 8)
+    g.vector.wait_ge(M.pv, 2)
+    g.scalar.wait_ge(M.ec, 8)
+    g.scalar.wait_ge(M.pv, 2)
+    for base, eng, done, out in ((0, g.vector, M.vc, M.vo), (4, g.scalar, M.sc, M.so)):
+        for i in range(4):
+            o = base + i
+            eng.wait_ge(M.lm, turn.index(o) + 1)
+            src, dst = T.P[:, 512 * o + 128 - fw:512 * o + 128], T.S[:, KP * o + hw:KP * o + KP]
+            if base:
+                eng.activation(dst, src, COPY).then_inc(done, 1)
+            else:
+                eng.tensor_copy(dst, src).then_inc(done, 1)
+            if i == 0:
+                continue
+            eng.wait_ge(done, i + 1)
+            f, m = (o - 1, 2) if i == 1 else (o, 1)
+            win = T.S[:, KP * f:KP * (f + m)].indirect(T.V[:, 0:J * m])
+            yo = T.YS[:, CW * f:CW * (f + m)]
+            if base:
+                eng.activation(yo, win, COPY).then_inc(out, 1)
+            else:
+                eng.tensor_copy(yo, win).then_inc(out, 1)
+    for lo, sem, v in ((0, M.vo, 1), (4, M.so, 1), (2, M.vo, 3), (6, M.so, 3)):
+        g.sync.wait_ge(sem, v)
+        g.sync.dma_start(T.y[:, CW * lo:CW * (lo + 2)], T.YS[:, CW * lo:CW * (lo + 2)]).then_inc(M.st, 16)
+    g.sync.wait_ge(M.st, 64)

@@ -8,6 +8,7 @@ CW = 128
 QT = 8
 PAD = 128 - CAPP
 NE = 128 + (N - 1) * CAPP
+PIECES = [(0, 4), (4, 6), (6, 8)]
 
 SCRATCH = {
     "L": ("sbuf", [128, KP // 16], "int32"),
@@ -26,12 +27,12 @@ SCRATCH = {
     "PLI": ("sbuf", [128, CW // 16], "int32"),
     "TM": ("sbuf", [128, N * (CW // 16)], "int32"),
     "AC": ("sbuf", [128, (N + 1) * (CW // 16)], "int32"),
-    "V": ("sbuf", [128, 2 * (CW // 16)], "uint16"),
+    "V": ("sbuf", [128, CW // 16], "uint16"),
     "S": ("sbuf", [128, QT * KP], "float32"),
     "YS": ("sbuf", [128, QT * CW], "float32"),
     "P": ("psum", [128, QT * 512], "float32"),
 }
-SEMAPHORES = ["lst", "xin", "qa", "qb", "pls", "vz", "vl", "vg", "sg", "qx", "ex", "wq", "vp", "sent", "loc",
+SEMAPHORES = ["lst", "xin", "q0", "q1", "q2", "pls", "vz", "vl", "vg", "sg", "qx", "ex", "wq", "vp", "locf", "loc",
               "near", "far", "rc", "rs", "em", "ec", "lm", "vc", "sc", "vo", "so", "pv", "st"]
 
 
@@ -103,12 +104,14 @@ def owner_program(g, core, T, topo, rank):
     COPY = ActivationFunctionType.Copy
 
     for p in range(8):
-        q = g.sync if p < 3 else g.scalar
+        q = g.sync if p < 4 else g.scalar
         q.dma_start(T.L[16 * p:16 * p + 16, :], T.snd[:, :]).then_inc(M.lst, 16)
     g.sync.dma_start(T.X[:, :], T.x[:, :]).then_inc(M.xin, 16)
-    g.sync.dma_start(T.WQ[:, 0:2048], T.qw[:, 0:2048]).then_inc(M.qa, 16)
+    for k in (0, 1):
+        a, b = PIECES[k]
+        g.sync.dma_start(T.WQ[:, 512 * a:512 * b], T.qw[:, 512 * a:512 * b]).then_inc(M["q%d" % k], 16)
     for p in range(8):
-        g.scalar.dma_start(T.PLI[16 * p:16 * p + 16, :], T.pl[:, :]).then_inc(M.pls, 16)
+        g.sync.dma_start(T.PLI[16 * p:16 * p + 16, :], T.pl[:, :]).then_inc(M.pls, 16)
 
     h0 = 4 * PAD
     h1 = h0 + 4 * KP
@@ -152,21 +155,26 @@ def owner_program(g, core, T, topo, rank):
         nc.append(send(topo, core, d, e, M.near, T.QC[:, a:a + CAPP].bitcast(dt.uint8), T.EC[:, b:b + CAPP].bitcast(dt.uint8)))
         ns.append(send(topo, core, d, e, M.near, T.QS[:, a:a + CAPP], T.ES[:, b:b + CAPP]))
     g.wait_ge(M.qx, 1)
-    g.remote_dma_fused(fc, local_sem=M.loc)
-    g.remote_dma_fused(fs, local_sem=M.loc)
-    g.sem_inc(M.sent, 1)
+    g.remote_dma_fused(fc, local_sem=M.locf)
+    g.remote_dma_fused(fs, local_sem=M.locf)
     g.remote_dma_fused(nc, local_sem=M.loc)
     g.remote_dma_fused(ns, local_sem=M.loc)
-    g.wait_ge(M.loc, 64)
+    g.wait_ge(M.loc, 32)
 
-    g.sync.wait_ge(M.sent, 1)
-    g.sync.dma_start(T.WQ[:, 2048:4096], T.qw[:, 2048:4096]).then_inc(M.qb, 16)
+    a, b = PIECES[2]
+    g.sync.wait_ge(M.locf, 32)
+    g.sync.dma_start(T.WQ[:, 512 * a:512 * b], T.qw[:, 512 * a:512 * b]).then_inc(M.q2, 16)
 
     s0 = 4 * (rank * CAPP)
     g.vector.wait_ge(M.vz, 1)
     g.vector.quantize_mx(T.EC[:, 0:128], T.ES[:, 0:128], T.H[:, s0:s0 + 512]).then_inc(M.ex, 1)
-    g.vector.wait_ge(M.qa, 16)
-    g.vector.quantize_mx(T.WC[:, 0:512], T.WS[:, 0:512], T.WQ[:, 0:2048]).then_inc(M.wq, 1)
+
+    def pack(k):
+        a, b = PIECES[k]
+        g.vector.wait_ge(M["q%d" % k], 16)
+        g.vector.quantize_mx(T.WC[:, 128 * a:128 * b], T.WS[:, 128 * a:128 * b], T.WQ[:, 512 * a:512 * b]).then_inc(M.wq, 1)
+    pack(0)
+    pack(1)
 
     order = [rank] + near + far
     delta = [CAPP * (order.index(q) - q) for q in range(N)]
@@ -177,61 +185,56 @@ def owner_program(g, core, T, topo, rank):
         g.vector.tensor_scalar(T.TM[:, J * i:J * i + J], T.PLI[:, :], q * CAPP, s, AluOpType.is_ge, AluOpType.mult).then_inc(M.vp, 1)
     n = 1 + len(steps)
     for i in range(len(steps)):
+        out = T.V[:, 0:J] if i + 1 == len(steps) else T.AC[:, J * (i + 1):J * (i + 2)]
         g.vector.wait_ge(M.vp, n)
         g.vector.tensor_tensor(T.AC[:, J * (i + 1):J * (i + 2)], T.AC[:, J * i:J * (i + 1)], T.TM[:, J * i:J * i + J],
                                AluOpType.add).then_inc(M.vp, 1)
         n += 1
-    last = T.AC[:, J * len(steps):J * (len(steps) + 1)]
     g.vector.wait_ge(M.vp, n)
-    g.vector.tensor_scalar(T.V[:, 0:J], last, 0, None, AluOpType.add).then_inc(M.pv, 1)
-    g.vector.tensor_scalar(T.V[:, J:2 * J], last, KP, None, AluOpType.add).then_inc(M.pv, 1)
-    g.vector.wait_ge(M.qb, 16)
-    g.vector.quantize_mx(T.WC[:, 512:1024], T.WS[:, 512:1024], T.WQ[:, 2048:4096]).then_inc(M.wq, 1)
+    g.vector.tensor_copy(T.V[:, 0:J], T.AC[:, J * len(steps):J * (len(steps) + 1)]).then_inc(M.pv, 1)
+    pack(2)
 
-    e0 = 128 + len(near) * CAPP - 128
+    e0 = len(near) * CAPP
     l0 = NE - 128
     hw = (1 + len(near)) * CAPP
     fw = len(far) * CAPP
+
+    def product(o, c0, sem):
+        g.tensor.matmul_mx(T.P[:, 512 * o:512 * o + 128], T.WC[:, 128 * o:128 * o + 128], T.WS[:, 128 * o:128 * o + 128],
+                           T.EC[:, c0:c0 + 128], T.ES[:, c0:c0 + 128], True, True).then_inc(sem, 1)
     g.tensor.wait_ge(M.ex, 1)
     g.tensor.wait_ge(M.near, 32)
-    for o in range(QT):
-        if o % 4 == 0:
-            g.tensor.wait_ge(M.wq, o // 4 + 1)
-        g.tensor.matmul_mx(T.P[:, 512 * o:512 * o + 128], T.WC[:, 128 * o:128 * o + 128], T.WS[:, 128 * o:128 * o + 128],
-                           T.EC[:, e0:e0 + 128], T.ES[:, e0:e0 + 128], True, True).then_inc(M.em, 1)
-        g.scalar.wait_ge(M.em, o + 1)
-        g.scalar.activation(T.S[:, KP * o:KP * o + hw], T.P[:, 512 * o + 128 - hw:512 * o + 128], COPY).then_inc(M.ec, 1)
-    turn = [0, 4, 1, 5, 2, 6, 3, 7]
+    for k in range(3):
+        g.tensor.wait_ge(M.wq, k + 1)
+        for o in range(*PIECES[k]):
+            product(o, e0, M.em)
+            g.scalar.wait_ge(M.em, o + 1)
+            g.scalar.activation(T.S[:, KP * o:KP * o + hw], T.P[:, 512 * o + 128 - hw:512 * o + 128], COPY).then_inc(M.ec, 1)
     g.tensor.wait_ge(M.far, 32)
     g.tensor.wait_ge(M.ec, 8)
-    for o in turn:
-        g.tensor.matmul_mx(T.P[:, 512 * o:512 * o + 128], T.WC[:, 128 * o:128 * o + 128], T.WS[:, 128 * o:128 * o + 128],
-                           T.EC[:, l0:l0 + 128], T.ES[:, l0:l0 + 128], True, True).then_inc(M.lm, 1)
+    for o in range(QT):
+        product(o, l0, M.lm)
 
     g.vector.wait_ge(M.ec, 8)
-    g.vector.wait_ge(M.pv, 2)
+    g.vector.wait_ge(M.pv, 1)
     g.scalar.wait_ge(M.ec, 8)
-    g.scalar.wait_ge(M.pv, 2)
-    for base, eng, done, out in ((0, g.vector, M.vc, M.vo), (4, g.scalar, M.sc, M.so)):
-        for i in range(4):
-            o = base + i
-            eng.wait_ge(M.lm, turn.index(o) + 1)
-            src, dst = T.P[:, 512 * o + 128 - fw:512 * o + 128], T.S[:, KP * o + hw:KP * o + KP]
-            if base:
-                eng.activation(dst, src, COPY).then_inc(done, 1)
-            else:
-                eng.tensor_copy(dst, src).then_inc(done, 1)
-            if i == 0:
-                continue
-            eng.wait_ge(done, i + 1)
-            f, m = (o - 1, 2) if i == 1 else (o, 1)
-            win = T.S[:, KP * f:KP * (f + m)].indirect(T.V[:, 0:J * m])
-            yo = T.YS[:, CW * f:CW * (f + m)]
-            if base:
-                eng.activation(yo, win, COPY).then_inc(out, 1)
-            else:
-                eng.tensor_copy(yo, win).then_inc(out, 1)
-    for lo, sem, v in ((0, M.vo, 1), (4, M.so, 1), (2, M.vo, 3), (6, M.so, 3)):
-        g.sync.wait_ge(sem, v)
-        g.sync.dma_start(T.y[:, CW * lo:CW * (lo + 2)], T.YS[:, CW * lo:CW * (lo + 2)]).then_inc(M.st, 16)
+    g.scalar.wait_ge(M.pv, 1)
+    for o in range(QT):
+        src, dst = T.P[:, 512 * o + 128 - fw:512 * o + 128], T.S[:, KP * o + hw:KP * o + KP]
+        win = T.S[:, KP * o:KP * o + KP].indirect(T.V[:, 0:J])
+        yo = T.YS[:, CW * o:CW * o + CW]
+        if o % 2 == 0:
+            g.vector.wait_ge(M.lm, o + 1)
+            g.vector.tensor_copy(dst, src).then_inc(M.vc, 1)
+            g.vector.wait_ge(M.vc, o // 2 + 1)
+            g.vector.tensor_copy(yo, win).then_inc(M.vo, 1)
+        else:
+            g.scalar.wait_ge(M.lm, o + 1)
+            g.scalar.activation(dst, src, COPY).then_inc(M.sc, 1)
+            g.scalar.wait_ge(M.sc, o // 2 + 1)
+            g.scalar.activation(yo, win, COPY).then_inc(M.so, 1)
+    for i in range(QT // 2):
+        g.sync.wait_ge(M.vo, i + 1)
+        g.sync.wait_ge(M.so, i + 1)
+        g.sync.dma_start(T.y[:, 2 * CW * i:2 * CW * (i + 1)], T.YS[:, 2 * CW * i:2 * CW * (i + 1)]).then_inc(M.st, 16)
     g.sync.wait_ge(M.st, 64)

@@ -6,20 +6,27 @@ KP = 160
 CAPP = KP // N
 CW = 128
 QT = 8
-PAD = 128 - CAPP
+LC = 3
+HC = 16 * LC
+PADF = 128 - 2 * HC
+PADN = 128 - CAPP
 NE = 128 + (N - 1) * CAPP
 PIECES = [(0, 4), (4, 6), (6, 8)]
 
 SCRATCH = {
     "L": ("sbuf", [128, KP // 16], "int32"),
-    "U": ("sbuf", [128, 4 * (KP // 16)], "uint16"),
+    "UF": ("sbuf", [128, 8 * LC], "uint16"),
+    "UN": ("sbuf", [128, 8 * LC], "uint16"),
     "X": ("sbuf", [128, 1024], "bfloat16"),
-    "H": ("sbuf", [128, 4 * (PAD + KP)], "bfloat16"),
+    "HF": ("sbuf", [128, 4 * (PADF + 2 * HC)], "bfloat16"),
+    "HN": ("sbuf", [128, 4 * (PADN + 2 * HC)], "bfloat16"),
     "WQ": ("sbuf", [128, QT * 512], "bfloat16"),
     "WC": ("sbuf", [128, QT * 128], "float8_e4m3fn_x4"),
     "WS": ("sbuf", [128, QT * 128], "uint8"),
-    "QC": ("sbuf", [128, KP], "float8_e4m3fn_x4"),
-    "QS": ("sbuf", [128, KP], "uint8"),
+    "FC": ("sbuf", [128, 128], "float8_e4m3fn_x4"),
+    "FS": ("sbuf", [128, 128], "uint8"),
+    "NC": ("sbuf", [128, 128], "float8_e4m3fn_x4"),
+    "NS": ("sbuf", [128, 128], "uint8"),
     "EC": ("sbuf", [128, NE], "float8_e4m3fn_x4"),
     "ES": ("sbuf", [128, NE], "uint8"),
     "RC": ("sbuf", [128, 2 * CAPP], "float8_e4m3fn_x4"),
@@ -32,26 +39,47 @@ SCRATCH = {
     "YS": ("sbuf", [128, QT * CW], "float32"),
     "P": ("psum", [128, QT * 512], "float32"),
 }
-SEMAPHORES = ["lst", "xin", "q0", "q1", "q2", "pls", "vz", "vl", "vg", "sg", "qx", "ex", "wq", "vp", "locf", "loc",
-              "near", "far", "rc", "rs", "em", "ec", "lm", "vc", "sc", "vo", "so", "pv", "st"]
+SEMAPHORES = ["lst", "xin", "q0", "q1", "q2", "pls", "vz", "vy", "vl", "vn", "vg", "sg", "hg", "tg", "qf", "qn", "ex", "wq", "vp",
+              "loc", "near", "far", "rc", "rs", "em", "ec", "lm", "vc", "sc", "vo", "so", "pv", "st"]
+
+
+def by_chip(T, topo, ranks):
+    groups = []
+    for q in sorted(ranks):
+        if groups and T.cores[q] in topo.cores_of(T.cores[groups[-1][-1]]):
+            groups[-1].append(q)
+        else:
+            groups.append([q])
+    return groups
 
 
 def near_far(T, topo, core):
     near = [q for q in range(N) if T.cores[q] != core and topo.may_write(core, T.cores[q])]
     far = [q for q in range(N) if T.cores[q] != core and q not in near]
-    groups = []
-    for q in far:
-        if groups and T.cores[q] in topo.cores_of(T.cores[groups[-1][-1]]):
-            groups[-1].append(q)
-        else:
-            groups.append([q])
-    return near, far, groups
+    here = [q for q in range(N) if T.cores[q] in topo.cores_of(core)]
+    return near, far, here
 
 
-def relays(T, topo, core, groups):
-    ports = [k for k in topo.cores_of(core) if topo.die(k) == topo.die(core) and T.rank_of(k) is None
-             and topo.may_write(k, T.cores[groups[0][0]])]
-    return ports[:len(groups)]
+def part(e, i, n):
+    w = len(e) // n
+    return e[i * w:(i + 1) * w]
+
+
+def ports(T, topo, core):
+    near, far, here = near_far(T, topo, core)
+    own = [k for k in topo.cores_of(core) if T.rank_of(k) is None and topo.may_write(k, T.cores[far[0]])]
+    away = [q for q in near if topo.same_plane(core, T.cores[q])]
+    outer = topo.engines(core, T.cores[away[0]])
+    inner = [e for e in topo.engines(core, own[0]) if e not in outer]
+    mine = [k for k in own if topo.die(k) == topo.die(core)]
+    groups = by_chip(T, topo, far)
+    planes = [(mine[i], gr, part(inner, i, len(groups))) for i, gr in enumerate(groups)]
+    codes, taken = [], []
+    for i, q in enumerate(far):
+        port = [k for k in own if topo.die(k) == topo.die(T.cores[q]) and k not in taken][0]
+        taken.append(port)
+        codes.append((port, q, part(inner, i, len(far))))
+    return planes, codes
 
 
 def bits(engines):
@@ -65,116 +93,159 @@ def send(topo, src, dst, engines, sem, frm, to):
 
 def rank_program(g, core, T, topo):
     rank = T.rank_of(core)
-    if rank is None:
-        for owner in T.cores:
-            if owner in topo.cores_of(core):
-                near, far, groups = near_far(T, topo, owner)
-                ports = relays(T, topo, owner, groups)
-                if core in ports:
-                    relay_program(g, core, T, topo, T.rank_of(owner), groups[ports.index(core)])
+    if rank is not None:
+        owner_program(g, core, T, topo, rank)
         return
-    owner_program(g, core, T, topo, rank)
+    owners = [c for c in T.cores if c in topo.cores_of(core)]
+    if owners and any(core == r[0] for r in ports(T, topo, owners[0])[1]):
+        relay_program(g, core, T, topo, owners)
 
 
-def relay_program(g, core, T, topo, src, dsts):
+def landing(T, topo, d, src):
+    near, far, here = near_far(T, topo, d)
+    return 128 + (len(near) + far.index(src)) * CAPP
+
+
+def relay_program(g, core, T, topo, owners):
     M = T.sem
-    codes, planes = [], []
-    for i, q in enumerate(dsts):
-        d = T.cores[q]
-        n, f, gr = near_far(T, topo, d)
-        e = topo.engines(core, d)
-        w = len(e) // len(dsts)
-        e = e[i * w:(i + 1) * w]
-        a, b = i * CAPP, 128 + (len(n) + f.index(src)) * CAPP
-        codes.append(send(topo, core, d, e, M.far, T.RC[:, a:a + CAPP].bitcast(dt.uint8), T.EC[:, b:b + CAPP].bitcast(dt.uint8)))
-        planes.append(send(topo, core, d, e, M.far, T.RS[:, a:a + CAPP], T.ES[:, b:b + CAPP]))
-    g.wait_ge(M.rc, 8)
-    g.remote_dma_fused(codes, local_sem=M.loc)
-    g.wait_ge(M.rs, 8)
+    planes, codes, wp, wc, left = [], [], 0, 0, 0
+    for c in owners:
+        src = T.rank_of(c)
+        pl, co = ports(T, topo, c)
+        for port, gr, e in pl:
+            if port == core:
+                wp += len(e)
+                for i, q in enumerate(gr):
+                    d = T.cores[q]
+                    a, b = i * CAPP, landing(T, topo, d, src)
+                    es = part(topo.engines(core, d), i, len(gr))
+                    left += len(es)
+                    planes.append(send(topo, core, d, es, M.far, T.RS[:, a:a + CAPP], T.ES[:, b:b + CAPP]))
+        for port, q, e in co:
+            if port == core:
+                wc += len(e)
+                d = T.cores[q]
+    n, b = len(owners) * CAPP, landing(T, topo, d, T.rank_of(owners[0]))
+    es = topo.engines(core, d)
+    codes.append(send(topo, core, d, es, M.far, T.RC[:, 0:n].bitcast(dt.uint8), T.EC[:, b:b + n].bitcast(dt.uint8)))
+    g.wait_ge(M.rs, wp)
     g.remote_dma_fused(planes, local_sem=M.loc)
-    g.wait_ge(M.loc, 16)
+    g.wait_ge(M.rc, wc)
+    g.remote_dma_fused(codes, local_sem=M.loc)
+    g.wait_ge(M.loc, left + len(es))
+
+
+def far_increments(T, topo, core, rank):
+    far = near_far(T, topo, core)[1]
+    n = 0
+    for q in far:
+        pl, co = ports(T, topo, T.cores[q])
+        for port, gr, e in pl:
+            if rank in gr:
+                n += len(part(topo.engines(port, core), gr.index(rank), len(gr)))
+    for gr in by_chip(T, topo, far):
+        n += sum(len(topo.engines(port, core)) for port, q, e in ports(T, topo, T.cores[gr[0]])[1] if q == rank)
+    return n
 
 
 def owner_program(g, core, T, topo, rank):
     M = T.sem
-    near, far, groups = near_far(T, topo, core)
-    ports = relays(T, topo, core, groups)
-    K = KP // 16
+    near, far, here = near_far(T, topo, core)
+    fgr = by_chip(T, topo, far)
+    ngr = by_chip(T, topo, near + [rank])
+    K = 2 * LC
     J = CW // 16
     COPY = ActivationFunctionType.Copy
+
+    def first(gr):
+        return gr[0] * CAPP // 16
+
+    def place(gs, pad, q):
+        i = [k for k, gr in enumerate(gs) if q in gr][0]
+        return pad + HC * i + q * CAPP - 16 * first(gs[i])
 
     for p in range(8):
         q = g.sync if p < 4 else g.scalar
         q.dma_start(T.L[16 * p:16 * p + 16, :], T.snd[:, :]).then_inc(M.lst, 16)
     g.sync.dma_start(T.X[:, :], T.x[:, :]).then_inc(M.xin, 16)
-    for k in (0, 1):
-        a, b = PIECES[k]
+    for k, (a, b) in enumerate(PIECES):
         g.sync.dma_start(T.WQ[:, 512 * a:512 * b], T.qw[:, 512 * a:512 * b]).then_inc(M["q%d" % k], 16)
     for p in range(8):
         g.sync.dma_start(T.PLI[16 * p:16 * p + 16, :], T.pl[:, :]).then_inc(M.pls, 16)
 
-    h0 = 4 * PAD
-    h1 = h0 + 4 * KP
-    g.vector.memset(T.H[:, 0:h0], 0.0).then_inc(M.vz, 1)
+    g.vector.memset(T.HF[:, 0:4 * PADF], 0.0).then_inc(M.vz, 1)
+    g.vector.memset(T.HN[:, 0:4 * PADN], 0.0).then_inc(M.vy, 1)
+
+    def lists(U, gs, sem):
+        for i, gr in enumerate(gs):
+            c = first(gr)
+            g.vector.tensor_scalar(U[:, LC * i:LC * i + LC], T.L[:, c:c + LC], 4, None, AluOpType.mult).then_inc(sem, 1)
+        g.vector.wait_ge(sem, 2)
+        for t in (2, 1, 3):
+            g.vector.tensor_scalar(U[:, K * t:K * t + K], U[:, 0:K], t, None, AluOpType.add).then_inc(sem, 1)
+
+    def gathers(U, H, pad, lsem, vsem, ssem):
+        h0, h1 = 4 * pad, 4 * (pad + 2 * HC)
+        for i, t in enumerate((0, 2)):
+            g.scalar.wait_ge(lsem, 2 + i)
+            g.scalar.activation(H[:, h0 + t:h1:4], T.X[:, 0:1024].indirect(U[:, K * t:K * t + K]), COPY).then_inc(ssem, 1)
+        for i, t in enumerate((1, 3)):
+            g.vector.wait_ge(lsem, 4 + i)
+            g.vector.tensor_copy(H[:, h0 + t:h1:4], T.X[:, 0:1024].indirect(U[:, K * t:K * t + K])).then_inc(vsem, 1)
+        g.vector.wait_ge(vsem, 2)
+        g.vector.wait_ge(ssem, 2)
+
     g.vector.wait_ge(M.lst, 128)
-    for t in (2, 3, 0, 1):
-        g.vector.tensor_scalar(T.U[:, K * t:K * t + K], T.L[:, :], 4, t, AluOpType.mult, AluOpType.add).then_inc(M.vl, 1)
+    lists(T.UF, fgr, M.vl)
     g.scalar.wait_ge(M.xin, 16)
-    for i, t in enumerate((2, 3)):
-        g.scalar.wait_ge(M.vl, i + 1)
-        g.scalar.activation(T.H[:, h0 + t:h1:4], T.X[:, 0:1024].indirect(T.U[:, K * t:K * t + K]), COPY).then_inc(M.sg, 1)
     g.vector.wait_ge(M.xin, 16)
-    for i, t in enumerate((0, 1)):
-        g.vector.wait_ge(M.vl, i + 3)
-        g.vector.tensor_copy(T.H[:, h0 + t:h1:4], T.X[:, 0:1024].indirect(T.U[:, K * t:K * t + K])).then_inc(M.vg, 1)
-    g.vector.wait_ge(M.vg, 2)
-    g.vector.wait_ge(M.sg, 2)
-    g.vector.quantize_mx(T.QC[:, 0:KP], T.QS[:, 0:KP], T.H[:, h0:h1]).then_inc(M.qx, 1)
+    gathers(T.UF, T.HF, PADF, M.vl, M.vg, M.sg)
+    g.vector.wait_ge(M.vz, 1)
+    g.vector.quantize_mx(T.FC[:, 0:128], T.FS[:, 0:128], T.HF[:, 0:512]).then_inc(M.qf, 1)
+
+    lists(T.UN, ngr, M.vn)
+    gathers(T.UN, T.HN, PADN, M.vn, M.hg, M.tg)
+    g.vector.wait_ge(M.vy, 1)
+    n0 = PADN + 2 * HC - 128
+    g.vector.quantize_mx(T.NC[:, 0:128], T.NS[:, 0:128], T.HN[:, 4 * n0:4 * n0 + 512]).then_inc(M.qn, 1)
+    s0 = 4 * (place(ngr, PADN, rank) + CAPP - 128)
+    g.vector.quantize_mx(T.EC[:, 0:128], T.ES[:, 0:128], T.HN[:, s0:s0 + 512]).then_inc(M.ex, 1)
 
     fc, fs, nc, ns = [], [], [], []
-    for i, gr in enumerate(groups):
-        e = topo.engines(core, ports[i])
-        w = len(e) // len(groups)
-        e = e[i * w:(i + 1) * w]
-        a = gr[0] * CAPP
-        b = a + len(gr) * CAPP
-        fc.append(send(topo, core, ports[i], e, M.rc, T.QC[:, a:b].bitcast(dt.uint8), T.RC[:, 0:b - a].bitcast(dt.uint8)))
-        fs.append(send(topo, core, ports[i], e, M.rs, T.QS[:, a:b], T.RS[:, 0:b - a]))
-    plane = [q for q in near if topo.same_plane(core, T.cores[q])]
+    sent = 0
+    planes, codes = ports(T, topo, core)
+    for port, gr, e in planes:
+        a, n = place(fgr, PADF, gr[0]), len(gr) * CAPP
+        sent += len(e)
+        fs.append(send(topo, core, port, e, M.rs, T.FS[:, a:a + n], T.RS[:, 0:n]))
+    r0 = here.index(rank) * CAPP
+    for port, q, e in codes:
+        a = place(fgr, PADF, q)
+        sent += len(e)
+        fc.append(send(topo, core, port, e, M.rc, T.FC[:, a:a + CAPP].bitcast(dt.uint8), T.RC[:, r0:r0 + CAPP].bitcast(dt.uint8)))
+    away = [q for q in near if topo.same_plane(core, T.cores[q])]
+    landed = 0
     for q in near:
         d = T.cores[q]
-        if q in plane:
-            e = topo.engines(core, d)
-            w = len(e) // len(plane)
-            i = plane.index(q)
-            e = e[i * w:(i + 1) * w]
+        if q in away:
+            e = part(topo.engines(core, d), away.index(q), len(away))
         else:
-            e = [k for k in topo.engines(core, d) if k not in topo.engines(core, T.cores[plane[0]])]
-        dn = near_far(T, topo, d)[0]
-        a, b = q * CAPP, 128 + dn.index(rank) * CAPP
-        nc.append(send(topo, core, d, e, M.near, T.QC[:, a:a + CAPP].bitcast(dt.uint8), T.EC[:, b:b + CAPP].bitcast(dt.uint8)))
-        ns.append(send(topo, core, d, e, M.near, T.QS[:, a:a + CAPP], T.ES[:, b:b + CAPP]))
-    g.wait_ge(M.qx, 1)
-    g.remote_dma_fused(fc, local_sem=M.locf)
-    g.remote_dma_fused(fs, local_sem=M.locf)
+            e = [k for k in topo.engines(core, d) if k not in topo.engines(core, T.cores[away[0]])]
+        landed += 2 * len(e)
+        a, b = place(ngr, PADN, q) - n0, 128 + near_far(T, topo, d)[0].index(rank) * CAPP
+        nc.append(send(topo, core, d, e, M.near, T.NC[:, a:a + CAPP].bitcast(dt.uint8), T.EC[:, b:b + CAPP].bitcast(dt.uint8)))
+        ns.append(send(topo, core, d, e, M.near, T.NS[:, a:a + CAPP], T.ES[:, b:b + CAPP]))
+    g.wait_ge(M.qf, 1)
+    g.remote_dma_fused(fs, local_sem=M.loc)
+    g.remote_dma_fused(fc, local_sem=M.loc)
+    g.wait_ge(M.qn, 1)
     g.remote_dma_fused(nc, local_sem=M.loc)
     g.remote_dma_fused(ns, local_sem=M.loc)
-    g.wait_ge(M.loc, 32)
+    g.wait_ge(M.loc, sent + landed)
 
-    a, b = PIECES[2]
-    g.sync.wait_ge(M.locf, 32)
-    g.sync.dma_start(T.WQ[:, 512 * a:512 * b], T.qw[:, 512 * a:512 * b]).then_inc(M.q2, 16)
-
-    s0 = 4 * (rank * CAPP)
-    g.vector.wait_ge(M.vz, 1)
-    g.vector.quantize_mx(T.EC[:, 0:128], T.ES[:, 0:128], T.H[:, s0:s0 + 512]).then_inc(M.ex, 1)
-
-    def pack(k):
-        a, b = PIECES[k]
+    for k, (a, b) in enumerate(PIECES):
         g.vector.wait_ge(M["q%d" % k], 16)
         g.vector.quantize_mx(T.WC[:, 128 * a:128 * b], T.WS[:, 128 * a:128 * b], T.WQ[:, 512 * a:512 * b]).then_inc(M.wq, 1)
-    pack(0)
-    pack(1)
 
     order = [rank] + near + far
     delta = [CAPP * (order.index(q) - q) for q in range(N)]
@@ -185,14 +256,12 @@ def owner_program(g, core, T, topo, rank):
         g.vector.tensor_scalar(T.TM[:, J * i:J * i + J], T.PLI[:, :], q * CAPP, s, AluOpType.is_ge, AluOpType.mult).then_inc(M.vp, 1)
     n = 1 + len(steps)
     for i in range(len(steps)):
-        out = T.V[:, 0:J] if i + 1 == len(steps) else T.AC[:, J * (i + 1):J * (i + 2)]
         g.vector.wait_ge(M.vp, n)
         g.vector.tensor_tensor(T.AC[:, J * (i + 1):J * (i + 2)], T.AC[:, J * i:J * (i + 1)], T.TM[:, J * i:J * i + J],
                                AluOpType.add).then_inc(M.vp, 1)
         n += 1
     g.vector.wait_ge(M.vp, n)
     g.vector.tensor_copy(T.V[:, 0:J], T.AC[:, J * len(steps):J * (len(steps) + 1)]).then_inc(M.pv, 1)
-    pack(2)
 
     e0 = len(near) * CAPP
     l0 = NE - 128
@@ -203,36 +272,49 @@ def owner_program(g, core, T, topo, rank):
         g.tensor.matmul_mx(T.P[:, 512 * o:512 * o + 128], T.WC[:, 128 * o:128 * o + 128], T.WS[:, 128 * o:128 * o + 128],
                            T.EC[:, c0:c0 + 128], T.ES[:, c0:c0 + 128], True, True).then_inc(sem, 1)
     g.tensor.wait_ge(M.ex, 1)
-    g.tensor.wait_ge(M.near, 32)
-    for k in range(3):
+    g.tensor.wait_ge(M.near, landed)
+    for k in range(len(PIECES)):
         g.tensor.wait_ge(M.wq, k + 1)
         for o in range(*PIECES[k]):
             product(o, e0, M.em)
             g.scalar.wait_ge(M.em, o + 1)
             g.scalar.activation(T.S[:, KP * o:KP * o + hw], T.P[:, 512 * o + 128 - hw:512 * o + 128], COPY).then_inc(M.ec, 1)
-    g.tensor.wait_ge(M.far, 32)
-    g.tensor.wait_ge(M.ec, 8)
+    g.tensor.wait_ge(M.far, far_increments(T, topo, core, rank))
     for o in range(QT):
+        g.tensor.wait_ge(M.ec, o + 1)
         product(o, l0, M.lm)
 
-    g.vector.wait_ge(M.ec, 8)
     g.vector.wait_ge(M.pv, 1)
-    g.scalar.wait_ge(M.ec, 8)
     g.scalar.wait_ge(M.pv, 1)
-    for o in range(QT):
+    g.scalar.wait_ge(M.ec, QT)
+
+    def copy(o, e):
         src, dst = T.P[:, 512 * o + 128 - fw:512 * o + 128], T.S[:, KP * o + hw:KP * o + KP]
+        e.wait_ge(M.lm, o + 1)
+        if e is g.scalar:
+            e.activation(dst, src, COPY).then_inc(M.sc, 1)
+        else:
+            e.wait_ge(M.ec, o + 1)
+            e.tensor_copy(dst, src).then_inc(M.vc, 1)
+
+    def pick(o, sem, n):
         win = T.S[:, KP * o:KP * o + KP].indirect(T.V[:, 0:J])
         yo = T.YS[:, CW * o:CW * o + CW]
         if o % 2 == 0:
-            g.vector.wait_ge(M.lm, o + 1)
-            g.vector.tensor_copy(dst, src).then_inc(M.vc, 1)
-            g.vector.wait_ge(M.vc, o // 2 + 1)
+            g.vector.wait_ge(sem, n)
             g.vector.tensor_copy(yo, win).then_inc(M.vo, 1)
         else:
-            g.scalar.wait_ge(M.lm, o + 1)
-            g.scalar.activation(dst, src, COPY).then_inc(M.sc, 1)
-            g.scalar.wait_ge(M.sc, o // 2 + 1)
+            g.scalar.wait_ge(sem, n)
             g.scalar.activation(yo, win, COPY).then_inc(M.so, 1)
+    for i in range(QT // 2 - 1):
+        copy(2 * i, g.vector)
+        pick(2 * i, M.vc, i + 1)
+        copy(2 * i + 1, g.scalar)
+        pick(2 * i + 1, M.sc, i + 1)
+    copy(QT - 2, g.vector)
+    copy(QT - 1, g.vector)
+    pick(QT - 2, M.vc, QT // 2)
+    pick(QT - 1, M.vc, QT // 2 + 1)
     for i in range(QT // 2):
         g.sync.wait_ge(M.vo, i + 1)
         g.sync.wait_ge(M.so, i + 1)

from concourse.bass import DstId, RemoteDMATransfer
from concourse.mybir import dt, AluOpType, ActivationFunctionType

N = 8
KP = 160
CAPP = KP // N
CW = 128
QT = 8
LC = 3
HC = 16 * LC
PADF = 128 - 2 * HC
PADN = 128 - CAPP
NE = 128 + (N - 1) * CAPP
PIECES = [(0, 4), (4, 6), (6, 8)]

SCRATCH = {
    "L": ("sbuf", [128, KP // 16], "int32"),
    "UF": ("sbuf", [128, 8 * LC], "uint16"),
    "UN": ("sbuf", [128, 8 * LC], "uint16"),
    "X": ("sbuf", [128, 1024], "bfloat16"),
    "HF": ("sbuf", [128, 4 * (PADF + 2 * HC)], "bfloat16"),
    "HN": ("sbuf", [128, 4 * (PADN + 2 * HC)], "bfloat16"),
    "WQ": ("sbuf", [128, QT * 512], "bfloat16"),
    "WC": ("sbuf", [128, QT * 128], "float8_e4m3fn_x4"),
    "WS": ("sbuf", [128, QT * 128], "uint8"),
    "FC": ("sbuf", [128, 128], "float8_e4m3fn_x4"),
    "FS": ("sbuf", [128, 128], "uint8"),
    "NC": ("sbuf", [128, 128], "float8_e4m3fn_x4"),
    "NS": ("sbuf", [128, 128], "uint8"),
    "EC": ("sbuf", [128, NE], "float8_e4m3fn_x4"),
    "ES": ("sbuf", [128, NE], "uint8"),
    "RC": ("sbuf", [128, 2 * CAPP], "float8_e4m3fn_x4"),
    "RS": ("sbuf", [128, 2 * CAPP], "uint8"),
    "PLI": ("sbuf", [128, CW // 16], "int32"),
    "TM": ("sbuf", [128, N * (CW // 16)], "int32"),
    "AC": ("sbuf", [128, (N + 1) * (CW // 16)], "int32"),
    "V": ("sbuf", [128, CW // 16], "uint16"),
    "S": ("sbuf", [128, QT * KP], "float32"),
    "YS": ("sbuf", [128, QT * CW], "float32"),
    "P": ("psum", [128, QT * 512], "float32"),
}
SEMAPHORES = ["lst", "xin", "q0", "q1", "q2", "pls", "vz", "vy", "vl", "vn", "vg", "sg", "hg", "tg", "qf", "qn", "ex", "wq", "vp",
              "loc", "near", "far", "rc", "rs", "em", "ec", "lm", "vc", "sc", "vo", "so", "pv", "st"]


def by_chip(T, topo, ranks):
    groups = []
    for q in sorted(ranks):
        if groups and T.cores[q] in topo.cores_of(T.cores[groups[-1][-1]]):
            groups[-1].append(q)
        else:
            groups.append([q])
    return groups


def near_far(T, topo, core):
    near = [q for q in range(N) if T.cores[q] != core and topo.may_write(core, T.cores[q])]
    far = [q for q in range(N) if T.cores[q] != core and q not in near]
    here = [q for q in range(N) if T.cores[q] in topo.cores_of(core)]
    return near, far, here


def part(e, i, n):
    w = len(e) // n
    return e[i * w:(i + 1) * w]


def ports(T, topo, core):
    near, far, here = near_far(T, topo, core)
    own = [k for k in topo.cores_of(core) if T.rank_of(k) is None and topo.may_write(k, T.cores[far[0]])]
    away = [q for q in near if topo.same_plane(core, T.cores[q])]
    outer = topo.engines(core, T.cores[away[0]])
    inner = [e for e in topo.engines(core, own[0]) if e not in outer]
    mine = [k for k in own if topo.die(k) == topo.die(core)]
    groups = by_chip(T, topo, far)
    planes = [(mine[i], gr, part(inner, i, len(groups))) for i, gr in enumerate(groups)]
    codes, taken = [], []
    for i, q in enumerate(far):
        port = [k for k in own if topo.die(k) == topo.die(T.cores[q]) and k not in taken][0]
        taken.append(port)
        codes.append((port, q, part(inner, i, len(far))))
    return planes, codes


def bits(engines):
    return sum(1 << e for e in engines)


def send(topo, src, dst, engines, sem, frm, to):
    rid, pid = topo.addr(dst, src)
    return RemoteDMATransfer(dst_ids=[DstId(rid=rid, pnc=pid)], dma_engine_mask=bits(engines), remote_sem=sem, src=frm, dst=to)


def rank_program(g, core, T, topo):
    rank = T.rank_of(core)
    if rank is not None:
        owner_program(g, core, T, topo, rank)
        return
    owners = [c for c in T.cores if c in topo.cores_of(core)]
    if owners and any(core == r[0] for r in ports(T, topo, owners[0])[1]):
        relay_program(g, core, T, topo, owners)


def landing(T, topo, d, src):
    near, far, here = near_far(T, topo, d)
    return 128 + (len(near) + far.index(src)) * CAPP


def relay_program(g, core, T, topo, owners):
    M = T.sem
    planes, codes, wp, wc, left = [], [], 0, 0, 0
    for c in owners:
        src = T.rank_of(c)
        pl, co = ports(T, topo, c)
        for port, gr, e in pl:
            if port == core:
                wp += len(e)
                for i, q in enumerate(gr):
                    d = T.cores[q]
                    a, b = i * CAPP, landing(T, topo, d, src)
                    es = part(topo.engines(core, d), i, len(gr))
                    left += len(es)
                    planes.append(send(topo, core, d, es, M.far, T.RS[:, a:a + CAPP], T.ES[:, b:b + CAPP]))
        for port, q, e in co:
            if port == core:
                wc += len(e)
                d = T.cores[q]
    n, b = len(owners) * CAPP, landing(T, topo, d, T.rank_of(owners[0]))
    es = topo.engines(core, d)
    codes.append(send(topo, core, d, es, M.far, T.RC[:, 0:n].bitcast(dt.uint8), T.EC[:, b:b + n].bitcast(dt.uint8)))
    g.wait_ge(M.rs, wp)
    g.remote_dma_fused(planes, local_sem=M.loc)
    g.wait_ge(M.rc, wc)
    g.remote_dma_fused(codes, local_sem=M.loc)
    g.wait_ge(M.loc, left + len(es))


def far_increments(T, topo, core, rank):
    far = near_far(T, topo, core)[1]
    n = 0
    for q in far:
        pl, co = ports(T, topo, T.cores[q])
        for port, gr, e in pl:
            if rank in gr:
                n += len(part(topo.engines(port, core), gr.index(rank), len(gr)))
    for gr in by_chip(T, topo, far):
        n += sum(len(topo.engines(port, core)) for port, q, e in ports(T, topo, T.cores[gr[0]])[1] if q == rank)
    return n


def owner_program(g, core, T, topo, rank):
    M = T.sem
    near, far, here = near_far(T, topo, core)
    fgr = by_chip(T, topo, far)
    ngr = by_chip(T, topo, near + [rank])
    K = 2 * LC
    J = CW // 16
    COPY = ActivationFunctionType.Copy

    def first(gr):
        return gr[0] * CAPP // 16

    def place(gs, pad, q):
        i = [k for k, gr in enumerate(gs) if q in gr][0]
        return pad + HC * i + q * CAPP - 16 * first(gs[i])

    for p in range(8):
        q = g.sync if p < 4 else g.scalar
        q.dma_start(T.L[16 * p:16 * p + 16, :], T.snd[:, :]).then_inc(M.lst, 16)
    g.sync.dma_start(T.X[:, :], T.x[:, :]).then_inc(M.xin, 16)
    for k, (a, b) in enumerate(PIECES):
        g.sync.dma_start(T.WQ[:, 512 * a:512 * b], T.qw[:, 512 * a:512 * b]).then_inc(M["q%d" % k], 16)
    for p in range(8):
        g.sync.dma_start(T.PLI[16 * p:16 * p + 16, :], T.pl[:, :]).then_inc(M.pls, 16)

    g.vector.memset(T.HF[:, 0:4 * PADF], 0.0).then_inc(M.vz, 1)
    g.vector.memset(T.HN[:, 0:4 * PADN], 0.0).then_inc(M.vy, 1)

    def lists(U, gs, sem):
        for i, gr in enumerate(gs):
            c = first(gr)
            g.vector.tensor_scalar(U[:, LC * i:LC * i + LC], T.L[:, c:c + LC], 4, None, AluOpType.mult).then_inc(sem, 1)
        g.vector.wait_ge(sem, 2)
        for t in (2, 1, 3):
            g.vector.tensor_scalar(U[:, K * t:K * t + K], U[:, 0:K], t, None, AluOpType.add).then_inc(sem, 1)

    def gathers(U, H, pad, lsem, vsem, ssem):
        h0, h1 = 4 * pad, 4 * (pad + 2 * HC)
        for i, t in enumerate((0, 2)):
            g.scalar.wait_ge(lsem, 2 + i)
            g.scalar.activation(H[:, h0 + t:h1:4], T.X[:, 0:1024].indirect(U[:, K * t:K * t + K]), COPY).then_inc(ssem, 1)
        for i, t in enumerate((1, 3)):
            g.vector.wait_ge(lsem, 4 + i)
            g.vector.tensor_copy(H[:, h0 + t:h1:4], T.X[:, 0:1024].indirect(U[:, K * t:K * t + K])).then_inc(vsem, 1)
        g.vector.wait_ge(vsem, 2)
        g.vector.wait_ge(ssem, 2)

    g.vector.wait_ge(M.lst, 128)
    lists(T.UF, fgr, M.vl)
    g.scalar.wait_ge(M.xin, 16)
    g.vector.wait_ge(M.xin, 16)
    gathers(T.UF, T.HF, PADF, M.vl, M.vg, M.sg)
    g.vector.wait_ge(M.vz, 1)
    g.vector.quantize_mx(T.FC[:, 0:128], T.FS[:, 0:128], T.HF[:, 0:512]).then_inc(M.qf, 1)

    lists(T.UN, ngr, M.vn)
    gathers(T.UN, T.HN, PADN, M.vn, M.hg, M.tg)
    g.vector.wait_ge(M.vy, 1)
    n0 = PADN + 2 * HC - 128
    g.vector.quantize_mx(T.NC[:, 0:128], T.NS[:, 0:128], T.HN[:, 4 * n0:4 * n0 + 512]).then_inc(M.qn, 1)
    s0 = 4 * (place(ngr, PADN, rank) + CAPP - 128)
    g.vector.quantize_mx(T.EC[:, 0:128], T.ES[:, 0:128], T.HN[:, s0:s0 + 512]).then_inc(M.ex, 1)

    fc, fs, nc, ns = [], [], [], []
    sent = 0
    planes, codes = ports(T, topo, core)
    for port, gr, e in planes:
        a, n = place(fgr, PADF, gr[0]), len(gr) * CAPP
        sent += len(e)
        fs.append(send(topo, core, port, e, M.rs, T.FS[:, a:a + n], T.RS[:, 0:n]))
    r0 = here.index(rank) * CAPP
    for port, q, e in codes:
        a = place(fgr, PADF, q)
        sent += len(e)
        fc.append(send(topo, core, port, e, M.rc, T.FC[:, a:a + CAPP].bitcast(dt.uint8), T.RC[:, r0:r0 + CAPP].bitcast(dt.uint8)))
    away = [q for q in near if topo.same_plane(core, T.cores[q])]
    landed = 0
    for q in near:
        d = T.cores[q]
        if q in away:
            e = part(topo.engines(core, d), away.index(q), len(away))
        else:
            e = [k for k in topo.engines(core, d) if k not in topo.engines(core, T.cores[away[0]])]
        landed += 2 * len(e)
        a, b = place(ngr, PADN, q) - n0, 128 + near_far(T, topo, d)[0].index(rank) * CAPP
        nc.append(send(topo, core, d, e, M.near, T.NC[:, a:a + CAPP].bitcast(dt.uint8), T.EC[:, b:b + CAPP].bitcast(dt.uint8)))
        ns.append(send(topo, core, d, e, M.near, T.NS[:, a:a + CAPP], T.ES[:, b:b + CAPP]))
    g.wait_ge(M.qf, 1)
    g.remote_dma_fused(fs, local_sem=M.loc)
    g.remote_dma_fused(fc, local_sem=M.loc)
    g.wait_ge(M.qn, 1)
    g.remote_dma_fused(nc, local_sem=M.loc)
    g.remote_dma_fused(ns, local_sem=M.loc)
    g.wait_ge(M.loc, sent + landed)

    for k, (a, b) in enumerate(PIECES):
        g.vector.wait_ge(M["q%d" % k], 16)
        g.vector.quantize_mx(T.WC[:, 128 * a:128 * b], T.WS[:, 128 * a:128 * b], T.WQ[:, 512 * a:512 * b]).then_inc(M.wq, 1)

    order = [rank] + near + far
    delta = [CAPP * (order.index(q) - q) for q in range(N)]
    steps = [(q, delta[q] - delta[q - 1]) for q in range(1, N) if delta[q] != delta[q - 1]]
    g.vector.wait_ge(M.pls, 128)
    g.vector.tensor_scalar(T.AC[:, 0:J], T.PLI[:, :], delta[0], None, AluOpType.add).then_inc(M.vp, 1)
    for i, (q, s) in enumerate(steps):
        g.vector.tensor_scalar(T.TM[:, J * i:J * i + J], T.PLI[:, :], q * CAPP, s, AluOpType.is_ge, AluOpType.mult).then_inc(M.vp, 1)
    n = 1 + len(steps)
    for i in range(len(steps)):
        g.vector.wait_ge(M.vp, n)
        g.vector.tensor_tensor(T.AC[:, J * (i + 1):J * (i + 2)], T.AC[:, J * i:J * (i + 1)], T.TM[:, J * i:J * i + J],
                               AluOpType.add).then_inc(M.vp, 1)
        n += 1
    g.vector.wait_ge(M.vp, n)
    g.vector.tensor_copy(T.V[:, 0:J], T.AC[:, J * len(steps):J * (len(steps) + 1)]).then_inc(M.pv, 1)

    e0 = len(near) * CAPP
    l0 = NE - 128
    hw = (1 + len(near)) * CAPP
    fw = len(far) * CAPP

    def product(o, c0, sem):
        g.tensor.matmul_mx(T.P[:, 512 * o:512 * o + 128], T.WC[:, 128 * o:128 * o + 128], T.WS[:, 128 * o:128 * o + 128],
                           T.EC[:, c0:c0 + 128], T.ES[:, c0:c0 + 128], True, True).then_inc(sem, 1)
    g.tensor.wait_ge(M.ex, 1)
    g.tensor.wait_ge(M.near, landed)
    for k in range(len(PIECES)):
        g.tensor.wait_ge(M.wq, k + 1)
        for o in range(*PIECES[k]):
            product(o, e0, M.em)
            g.scalar.wait_ge(M.em, o + 1)
            g.scalar.activation(T.S[:, KP * o:KP * o + hw], T.P[:, 512 * o + 128 - hw:512 * o + 128], COPY).then_inc(M.ec, 1)
    g.tensor.wait_ge(M.far, far_increments(T, topo, core, rank))
    for o in range(QT):
        g.tensor.wait_ge(M.ec, o + 1)
        product(o, l0, M.lm)

    g.vector.wait_ge(M.pv, 1)
    g.scalar.wait_ge(M.pv, 1)
    g.scalar.wait_ge(M.ec, QT)

    def copy(o, e):
        src, dst = T.P[:, 512 * o + 128 - fw:512 * o + 128], T.S[:, KP * o + hw:KP * o + KP]
        e.wait_ge(M.lm, o + 1)
        if e is g.scalar:
            e.activation(dst, src, COPY).then_inc(M.sc, 1)
        else:
            e.wait_ge(M.ec, o + 1)
            e.tensor_copy(dst, src).then_inc(M.vc, 1)

    def pick(o, sem, n):
        win = T.S[:, KP * o:KP * o + KP].indirect(T.V[:, 0:J])
        yo = T.YS[:, CW * o:CW * o + CW]
        if o % 2 == 0:
            g.vector.wait_ge(sem, n)
            g.vector.tensor_copy(yo, win).then_inc(M.vo, 1)
        else:
            g.scalar.wait_ge(sem, n)
            g.scalar.activation(yo, win, COPY).then_inc(M.so, 1)
    for i in range(QT // 2 - 1):
        copy(2 * i, g.vector)
        pick(2 * i, M.vc, i + 1)
        copy(2 * i + 1, g.scalar)
        pick(2 * i + 1, M.sc, i + 1)
    copy(QT - 2, g.vector)
    copy(QT - 1, g.vector)
    pick(QT - 2, M.vc, QT // 2)
    pick(QT - 1, M.vc, QT // 2 + 1)
    for i in range(QT // 2):
        g.sync.wait_ge(M.vo, i + 1)
        g.sync.wait_ge(M.so, i + 1)
        g.sync.dma_start(T.y[:, 2 * CW * i:2 * CW * (i + 1)], T.YS[:, 2 * CW * i:2 * CW * (i + 1)]).then_inc(M.st, 16)
    g.sync.wait_ge(M.st, 64)
